import numpy as np
import ml_dtypes


def mxq(x, axis, fmt="e4m3"):
    dtype, down = {"e4m3": (ml_dtypes.float8_e4m3fn, 7), "e5m2": (ml_dtypes.float8_e5m2, 14)}[fmt]
    v = np.moveaxis(np.asarray(x, np.float32).astype(ml_dtypes.bfloat16).astype(np.float64), axis, -1)
    blocks = v.reshape(v.shape[:-1] + (-1, 32))
    amax = np.abs(blocks).max(-1, keepdims=True)
    byte = np.maximum(np.where(amax > 0, np.frexp(amax)[1] - 1 + 127, 0) - down, 1)
    scale = np.exp2(byte - 127.0)
    codes = (blocks / scale).astype(np.float32).astype(dtype).astype(np.float64)
    return np.moveaxis((codes * scale).reshape(v.shape), -1, axis)


WIDE = False


def mx_kscale(k):
    if not WIDE:
        return np.ones(k)
    levels = np.array([10, -10, 5, -5, 0])
    if k % 512:
        return np.exp2(np.random.permutation(np.resize(levels, k // 32))).repeat(32)
    a = np.empty((k // 512, 16))
    for p in range(k // 512):
        a[p, :8] = np.random.permutation(np.resize(levels, 8))
        for g in range(8):
            far = levels[np.abs(levels - a[p, g]) >= 10]
            a[p, g + 8] = far[np.random.randint(len(far))]
    return np.exp2(a.ravel()).repeat(32)


def f64(x):
    return np.asarray(x).astype(np.float64)


def striped(idx):
    return np.tile(idx.reshape(-1, 16).T, (8, 1)).astype(np.uint16)


def unstriped(offs):
    return offs[:16].T.reshape(-1).astype(np.int64)


E2M1 = np.array([0.0, 0.5, 1.0, 1.5, 2.0, 3.0, 4.0, 6.0, -0.0, -0.5, -1.0, -1.5, -2.0, -3.0, -4.0, -6.0])


def pack_weight(w, fmt):
    k, n = w.shape
    w = f64(np.asarray(w, np.float32).astype(ml_dtypes.bfloat16)).reshape(k // 32, 32, n)
    amax = np.abs(w).max(1)
    if fmt == "e4m3":
        byte = np.frexp(amax)[1] - 1 + 127 - 7
    else:
        mant, ex = np.frexp(amax / 6.0)
        byte = np.where(mant > 0.5, ex, ex - 1) + 127
    byte = np.clip(np.where(amax > 0, byte, 1), 1, 254)
    scaled = (w * np.exp2(127.0 - byte)[:, None, :]).reshape(k, n).astype(np.float32)
    by_word = np.ascontiguousarray(scaled.reshape(k // 512, 128, 4, n).transpose(0, 1, 3, 2))
    if fmt == "e4m3":
        words = by_word.astype(ml_dtypes.float8_e4m3fn).view(np.uint8)
    else:
        c = by_word.astype(ml_dtypes.float4_e2m1fn).view(np.uint8) & 0xF
        words = (c[..., 0::2] | (c[..., 1::2] << 4)).reshape(k // 512, 128, 2 * n)
    return np.ascontiguousarray(words), np.ascontiguousarray(byte.astype(np.uint8).reshape(k // 512, 16, n))


def unpack_weight(words, scales, fmt):
    g, _, n = scales.shape
    words = np.ascontiguousarray(words).reshape(g, 128, n, -1)
    if fmt == "e4m3":
        vals = words.view(ml_dtypes.float8_e4m3fn).astype(np.float64)
    else:
        nib = np.empty((g, 128, n, 4), np.uint8)
        nib[..., 0::2] = words & 0xF
        nib[..., 1::2] = words >> 4
        vals = E2M1[nib]
    vals = vals * np.repeat(np.exp2(scales.astype(np.float64) - 127.0), 8, axis=1)[..., None]
    return vals.transpose(0, 1, 3, 2).reshape(g * 512, n)


K, T, E, N = 2560, 768, 6, 128
COUNTS = (128, 128, 128, 256, 384, 512)
STARTS = np.cumsum((0,) + COUNTS)


def by_expert(wq, xq):
    return np.concatenate([wq[e].T @ xq[:, STARTS[e]:STARTS[e + 1]] for e in range(E)], axis=1)


def setup_inputs():
    n = np.random.standard_normal
    s = mx_kscale(K)[:, None]
    both = np.repeat(np.arange(E), COUNTS)
    pair = np.stack([both[:T], both[T:]])[:, np.random.permutation(T)]
    pair = np.where(np.random.rand(T) < 0.5, pair, pair[::-1])
    order = np.argsort(pair.reshape(-1), kind="stable")
    slot_token = order % T; pos = np.empty(2 * T, np.int64); pos[order] = np.arange(2 * T); pos = pos.reshape(2, T)
    g = np.random.uniform(0.2, 0.8, T)
    w = [pack_weight(m, "e2m1") for m in n((E, K, N)) / np.sqrt(K) / s[None]]
    return {
        "xT": (n((K, T)) * s).astype(np.float32),
        "w_words": np.stack([m[0] for m in w]),
        "w_scales": np.stack([m[1] for m in w]),
        "b": (0.3 * n((N, E))).astype(np.float32),
        "gate": np.stack([np.tile(g, (N, 1)), np.tile(1.0 - g, (N, 1))]).astype(np.float32),
        "offs": striped(slot_token),
        "pos1": striped(pos[0]),
        "pos2": striped(pos[1]),
    }


def reference(xT, w_words, w_scales, b, gate, offs, pos1, pos2):
    idx = unstriped(offs)
    w = np.stack([unpack_weight(w_words[e], w_scales[e], "e2m1") for e in range(E)])
    xq = mxq(f64(xT)[:, idx], 0, "e4m3")
    y = by_expert(w, xq)
    y = y + np.repeat(f64(b), COUNTS, axis=1)
    return f64(gate[0]) * y[:, unstriped(pos1)] + f64(gate[1]) * y[:, unstriped(pos2)]

@@ -1,0 +1,216 @@
+from contextlib import ExitStack
+
+import concourse.mybir as mybir
+
+FLOPS = 2 * 1536 * 2560 * 128
+
+F32 = mybir.dt.float32
+BF16 = mybir.dt.bfloat16
+I32 = mybir.dt.int32
+U32 = mybir.dt.uint32
+U16 = mybir.dt.uint16
+U8 = mybir.dt.uint8
+FP8X4 = mybir.dt.float8_e4m3fn_x4
+FP4X4 = mybir.dt.float4_e2m1fn_x4
+MULT = mybir.AluOpType.mult
+IDENTITY = mybir.ActivationFunctionType.Identity
+
+P = 128
+T = 768
+S = 1536
+E = 6
+N = 128
+A = 5
+STARTS = (0, 128, 256, 384, 640, 1024, 1536)
+
+
+def tile_moe_rag_lin_bias_kernel(tc, xT, w_words, w_scales, b, gate, offs, pos1, pos2, out):
+    nc = tc.nc
+    with ExitStack() as ctx:
+        pool = ctx.enter_context(tc.tile_pool(name="held", bufs=1))
+        psum = ctx.enter_context(tc.psum_pool(name="psum", bufs=1))
+
+        def held(shape, dtype, name):
+            return pool.tile(shape, dtype, name=name, align_bytes=64)
+
+        offs_t = held([P, S // 16], U16, "offs_t")
+        pos1_t = held([P, T // 16], U16, "pos1_t")
+        pos2_t = held([P, T // 16], U16, "pos2_t")
+
+        chunks = [[(0, 256, "v"), (256, 256, "s"), (512, 256, "v")]]
+        for a in range(1, A):
+            chunks.append([(0, 512, "s"), (512, 256, "s")])
+
+        nc.sync.dma_start(offs_t[:], offs)
+        raws = {}
+        for a in range(A):
+            rows = xT[512 * a : 512 * (a + 1), :].rearrange("(p j) w -> p j w", j=4)
+            for t0, tn, eng in chunks[a]:
+                raw = held([P, 4, tn], F32, "raw_%d_%d" % (a, t0))
+                nc.sync.dma_start(out=raw[:], in_=rows[:, :, t0 : t0 + tn])
+                raws[(a, t0)] = raw
+
+        words = held([P, E * A * 2 * N], U8, "words")
+        wplane = held([P, E * A * N], U8, "wplane")
+        lone = held([P, T], U8, "lone")
+        packed = held([P, T], U8, "packed")
+        moved = {}
+        for a in (2, 3, 4):
+            moved[a] = held([P, S], U8, "moved_%d" % a)
+        for plane in (lone, packed, wplane, moved[2], moved[3], moved[4]):
+            nc.gpsimd.memset(plane[:].bitcast(I32), 0)
+
+        nc.sync.dma_start(
+            out=words[:].bitcast(I32).rearrange("p (m c) -> p m c", m=E * A),
+            in_=w_words.bitcast(I32).rearrange("e a p c -> p (e a) c"),
+        )
+        for q in range(4):
+            nc.sync.dma_start(
+                out=wplane[32 * q : 32 * q + 4, :].bitcast(I32).rearrange("r (m c) -> r m c", m=E * A),
+                in_=w_scales[:, :, 4 * q : 4 * q + 4, :].bitcast(I32).rearrange("e a r c -> r (e a) c"),
+            )
+        b_t = held([P, E], F32, "b_t")
+        nc.sync.dma_start(out=b_t[:], in_=b)
+        gates = []
+        for c in range(2):
+            g_t = held([P, T], F32, "gate_%d" % c)
+            nc.sync.dma_start(out=g_t[:], in_=gate[c])
+            gates.append(g_t)
+        nc.sync.dma_start(pos1_t[:], pos1)
+        nc.sync.dma_start(pos2_t[:], pos2)
+
+        codes = {}
+        gwords = {}
+        for a in range(A):
+            codes[a] = held([P, T], U32, "codes_%d" % a)
+            gwords[a] = held([P, S], U32, "gwords_%d" % a)
+        glone = held([P, S], U8, "glone")
+        gpacked = held([P, S], U8, "gpacked")
+
+        groups = {}
+
+        def cast(a):
+            for t0, tn, eng in chunks[a]:
+                grouped = held([P, tn, 4], BF16, "grouped_%d_%d" % (a, t0))
+                src = raws[(a, t0)][:].rearrange("p j w -> p w j")
+                if eng == "v":
+                    nc.vector.tensor_copy(out=grouped[:], in_=src)
+                else:
+                    nc.scalar.copy(out=grouped[:], in_=src)
+                groups[(a, t0)] = grouped
+
+        def quantize(a):
+            for t0, tn, eng in chunks[a]:
+                plane = lone[:, t0 : t0 + tn] if a == 0 else packed[4 * (a - 1) : P, t0 : t0 + tn]
+                nc.vector.quantize_mx(
+                    out=codes[a][:, t0 : t0 + tn].bitcast(FP8X4),
+                    scales=plane,
+                    in_=groups[(a, t0)][:].rearrange("p w j -> p (w j)"),
+                )
+
+        def gather(dst, src, s0, s1):
+            nc.vector.tensor_copy(dst[:, s0:s1], src[:].indirect(offs_t[:, s0 // 16 : s1 // 16]))
+
+        thirds = ((0, 512), (512, 1024), (1024, 1536))
+
+        for a in range(A):
+            cast(a)
+        quantize(0)
+        for s0, s1 in thirds:
+            gather(gwords[0], codes[0], s0, s1)
+        for s0, s1 in thirds:
+            gather(glone, lone, s0, s1)
+        for a in (1, 2):
+            quantize(a)
+            for s0, s1 in thirds:
+                gather(gwords[a], codes[a], s0, s1)
+        quantize(3)
+        quantize(4)
+        for s0, s1 in thirds:
+            gather(gpacked, packed, s0, s1)
+        for a in (2, 3, 4):
+            k = 4 * (a - 1)
+            nc.sync.dma_start(out=moved[a][0 : P - k, :].bitcast(I32), in_=gpacked[k:P, :].bitcast(I32))
+        planes = {0: glone, 1: gpacked, 2: moved[2], 3: moved[3], 4: moved[4]}
+
+        blocks = [
+            (7, 0, 5, 1024, 512),
+            (4, 0, 3, 512, 128),
+            (5, 0, 4, 640, 128),
+            (6, 0, 4, 768, 128),
+            (6, 128, 4, 896, 128),
+            (1, 0, 1, 128, 128),
+            (2, 0, 2, 256, 128),
+            (3, 0, 3, 384, 128),
+            (0, 0, 0, 0, 128),
+        ]
+        banks = []
+        for i in range(8):
+            banks.append(psum.tile([P, 512], F32, name="bank_%d" % i))
+        y = held([P, S], F32, "y")
+
+        def multiply(a, block):
+            bank, col, e, s0, sn = block
+            m = e * A + a
+            nc.tensor.matmul_mx(
+                out=banks[bank][:, col : col + sn],
+                lhsT=words[:, 2 * N * m : 2 * N * (m + 1)].bitcast(FP4X4),
+                lhsT_scale=wplane[:, N * m : N * (m + 1)],
+                rhs=gwords[a][:, s0 : s0 + sn].bitcast(FP8X4),
+                rhs_scale=planes[a][:, s0 : s0 + sn],
+                start=(a == 0),
+                stop=(a == A - 1),
+            )
+
+        def leave(bank, col, e, s0, sn):
+            nc.scalar.activation(out=y[:, s0 : s0 + sn], in_=banks[bank][:, col : col + sn], func=IDENTITY, bias=b_t[:, e : e + 1])
+
+        early = [blk for blk in blocks if blk[1] == 0]
+        for blk in early:
+            multiply(0, blk)
+        for blk in early:
+            multiply(1, blk)
+        for blk in early:
+            multiply(2, blk)
+        for s0, s1 in thirds:
+            gather(gwords[3], codes[3], s0, s1)
+        for blk in early:
+            multiply(3, blk)
+
+        for s0, s1 in ((1024, 1536), (512, 1024), (128, 512), (0, 128)):
+            gather(gwords[4], codes[4], s0, s1)
+            for blk in blocks:
+                if s0 <= blk[3] < s1:
+                    if blk[1] > 0:
+                        for a in range(A - 1):
+                            multiply(a, blk)
+                    multiply(4, blk)
+                    if blk[0] == 6:
+                        if blk[1] > 0:
+                            leave(6, 0, 4, 768, 256)
+                    else:
+                        leave(*blk)
+
+        cuts = ((0, 512), (512, 768))
+        terms = {}
+        for c, pos in ((0, pos1_t), (1, pos2_t)):
+            for t0, t1 in cuts:
+                terms[(c, t0)] = held([P, t1 - t0], F32, "term_%d_%d" % (c, t0))
+
+        def fetch(c, t0, t1):
+            pos = (pos1_t, pos2_t)[c]
+            nc.vector.tensor_tensor(
+                terms[(c, t0)][:], y[:].indirect(pos[:, t0 // 16 : t1 // 16]), gates[c][:, t0:t1], MULT
+            )
+
+        def finish(t0, t1):
+            total = held([P, t1 - t0], F32, "total_%d" % t0)
+            nc.vector.tensor_add(out=total[:], in0=terms[(0, t0)][:], in1=terms[(1, t0)][:])
+            nc.sync.dma_start(out=out[:, t0:t1], in_=total[:])
+
+        fetch(0, 0, 512)
+        fetch(1, 0, 512)
+        fetch(0, 512, 768)
+        finish(0, 512)
+        fetch(1, 512, 768)
+        finish(512, 768)

@@ -21,7 +21,6 @@ S = 1536
 E = 6
 N = 128
 A = 5
-STARTS = (0, 128, 256, 384, 640, 1024, 1536)
 
 
 def tile_moe_rag_lin_bias_kernel(tc, xT, w_words, w_scales, b, gate, offs, pos1, pos2, out):
@@ -37,8 +36,8 @@ def tile_moe_rag_lin_bias_kernel(tc, xT, w_words, w_scales, b, gate, offs, pos1,
         pos1_t = held([P, T // 16], U16, "pos1_t")
         pos2_t = held([P, T // 16], U16, "pos2_t")
 
-        chunks = [[(0, 256, "v"), (256, 256, "s"), (512, 256, "v")]]
-        for a in range(1, A):
+        chunks = [[(0, 256, "v"), (256, 256, "s"), (512, 256, "v")], [(0, 512, "s"), (512, 256, "v")]]
+        for a in range(2, A):
             chunks.append([(0, 512, "s"), (512, 256, "s")])
 
         nc.sync.dma_start(offs_t[:], offs)
@@ -55,22 +54,22 @@ def tile_moe_rag_lin_bias_kernel(tc, xT, w_words, w_scales, b, gate, offs, pos1,
         lone = held([P, T], U8, "lone")
         packed = held([P, T], U8, "packed")
         moved = {}
-        for a in (2, 3, 4):
+        for a in (1, 2, 3):
             moved[a] = held([P, S], U8, "moved_%d" % a)
-        for plane in (lone, packed, wplane, moved[2], moved[3], moved[4]):
+        for plane in (packed, lone, wplane, moved[1], moved[2], moved[3]):
             nc.gpsimd.memset(plane[:].bitcast(I32), 0)
 
-        nc.sync.dma_start(
-            out=words[:].bitcast(I32).rearrange("p (m c) -> p m c", m=E * A),
-            in_=w_words.bitcast(I32).rearrange("e a p c -> p (e a) c"),
-        )
+        b_t = held([P, E], F32, "b_t")
+        nc.sync.dma_start(out=b_t[:], in_=b)
         for q in range(4):
             nc.sync.dma_start(
                 out=wplane[32 * q : 32 * q + 4, :].bitcast(I32).rearrange("r (m c) -> r m c", m=E * A),
                 in_=w_scales[:, :, 4 * q : 4 * q + 4, :].bitcast(I32).rearrange("e a r c -> r (e a) c"),
             )
-        b_t = held([P, E], F32, "b_t")
-        nc.sync.dma_start(out=b_t[:], in_=b)
+        nc.sync.dma_start(
+            out=words[:].bitcast(I32).rearrange("p (m c) -> p m c", m=E * A),
+            in_=w_words.bitcast(I32).rearrange("e a p c -> p (e a) c"),
+        )
         gates = []
         for c in range(2):
             g_t = held([P, T], F32, "gate_%d" % c)
@@ -101,7 +100,7 @@ def tile_moe_rag_lin_bias_kernel(tc, xT, w_words, w_scales, b, gate, offs, pos1,
 
         def quantize(a):
             for t0, tn, eng in chunks[a]:
-                plane = lone[:, t0 : t0 + tn] if a == 0 else packed[4 * (a - 1) : P, t0 : t0 + tn]
+                plane = lone[:, t0 : t0 + tn] if a == A - 1 else packed[4 * a : P, t0 : t0 + tn]
                 nc.vector.quantize_mx(
                     out=codes[a][:, t0 : t0 + tn].bitcast(FP8X4),
                     scales=plane,
@@ -111,27 +110,7 @@ def tile_moe_rag_lin_bias_kernel(tc, xT, w_words, w_scales, b, gate, offs, pos1,
         def gather(dst, src, s0, s1):
             nc.vector.tensor_copy(dst[:, s0:s1], src[:].indirect(offs_t[:, s0 // 16 : s1 // 16]))
 
-        thirds = ((0, 512), (512, 1024), (1024, 1536))
-
-        for a in range(A):
-            cast(a)
-        quantize(0)
-        for s0, s1 in thirds:
-            gather(gwords[0], codes[0], s0, s1)
-        for s0, s1 in thirds:
-            gather(glone, lone, s0, s1)
-        for a in (1, 2):
-            quantize(a)
-            for s0, s1 in thirds:
-                gather(gwords[a], codes[a], s0, s1)
-        quantize(3)
-        quantize(4)
-        for s0, s1 in thirds:
-            gather(gpacked, packed, s0, s1)
-        for a in (2, 3, 4):
-            k = 4 * (a - 1)
-            nc.sync.dma_start(out=moved[a][0 : P - k, :].bitcast(I32), in_=gpacked[k:P, :].bitcast(I32))
-        planes = {0: glone, 1: gpacked, 2: moved[2], 3: moved[3], 4: moved[4]}
+        planes = {0: gpacked, 1: moved[1], 2: moved[2], 3: moved[3], 4: glone}
 
         blocks = [
             (7, 0, 5, 1024, 512),
@@ -144,6 +123,7 @@ def tile_moe_rag_lin_bias_kernel(tc, xT, w_words, w_scales, b, gate, offs, pos1,
             (3, 0, 3, 384, 128),
             (0, 0, 0, 0, 128),
         ]
+        early = [blk for blk in blocks if blk[1] == 0]
         banks = []
         for i in range(8):
             banks.append(psum.tile([P, 512], F32, name="bank_%d" % i))
@@ -163,21 +143,41 @@ def tile_moe_rag_lin_bias_kernel(tc, xT, w_words, w_scales, b, gate, offs, pos1,
             )
 
         def leave(bank, col, e, s0, sn):
-            nc.scalar.activation(out=y[:, s0 : s0 + sn], in_=banks[bank][:, col : col + sn], func=IDENTITY, bias=b_t[:, e : e + 1])
+            if s0 == 0:
+                nc.vector.tensor_scalar_add(out=y[:, s0 : s0 + sn], in0=banks[bank][:, col : col + sn], scalar1=b_t[:, e : e + 1])
+            else:
+                nc.scalar.activation(out=y[:, s0 : s0 + sn], in_=banks[bank][:, col : col + sn], func=IDENTITY, bias=b_t[:, e : e + 1])
 
-        early = [blk for blk in blocks if blk[1] == 0]
-        for blk in early:
-            multiply(0, blk)
-        for blk in early:
-            multiply(1, blk)
-        for blk in early:
-            multiply(2, blk)
+        thirds = ((0, 512), (512, 1024), (1024, 1536))
+
+        cast(0)
+        cast(1)
+        quantize(0)
+        for s0, s1 in thirds:
+            gather(gwords[0], codes[0], s0, s1)
+        cast(2)
+        quantize(1)
+        for s0, s1 in thirds:
+            gather(gwords[1], codes[1], s0, s1)
+        cast(3)
+        quantize(2)
+        for s0, s1 in thirds:
+            gather(gwords[2], codes[2], s0, s1)
+        cast(4)
+        quantize(3)
+        for s0, s1 in thirds:
+            gather(gpacked, packed, s0, s1)
+        for a in (1, 2, 3):
+            nc.sync.dma_start(out=moved[a][0 : P - 4 * a, :].bitcast(I32), in_=gpacked[4 * a : P, :].bitcast(I32))
         for s0, s1 in thirds:
             gather(gwords[3], codes[3], s0, s1)
-        for blk in early:
-            multiply(3, blk)
+        for a in range(4):
+            for blk in early:
+                multiply(a, blk)
+        quantize(4)
 
         for s0, s1 in ((1024, 1536), (512, 1024), (128, 512), (0, 128)):
+            gather(glone, lone, s0, s1)
             gather(gwords[4], codes[4], s0, s1)
             for blk in blocks:
                 if s0 <= blk[3] < s1:
@@ -191,17 +191,13 @@ def tile_moe_rag_lin_bias_kernel(tc, xT, w_words, w_scales, b, gate, offs, pos1,
                     else:
                         leave(*blk)
 
-        cuts = ((0, 512), (512, 768))
         terms = {}
-        for c, pos in ((0, pos1_t), (1, pos2_t)):
-            for t0, t1 in cuts:
-                terms[(c, t0)] = held([P, t1 - t0], F32, "term_%d_%d" % (c, t0))
 
         def fetch(c, t0, t1):
             pos = (pos1_t, pos2_t)[c]
-            nc.vector.tensor_tensor(
-                terms[(c, t0)][:], y[:].indirect(pos[:, t0 // 16 : t1 // 16]), gates[c][:, t0:t1], MULT
-            )
+            term = held([P, t1 - t0], F32, "term_%d_%d" % (c, t0))
+            nc.vector.tensor_tensor(term[:], y[:].indirect(pos[:, t0 // 16 : t1 // 16]), gates[c][:, t0:t1], MULT)
+            terms[(c, t0)] = term
 
         def finish(t0, t1):
             total = held([P, t1 - t0], F32, "total_%d" % t0)

@@ -36,18 +36,29 @@ def tile_moe_rag_lin_bias_kernel(tc, xT, w_words, w_scales, b, gate, offs, pos1,
         pos1_t = held([P, T // 16], U16, "pos1_t")
         pos2_t = held([P, T // 16], U16, "pos2_t")
 
-        chunks = [[(0, 256, "v"), (256, 256, "s"), (512, 256, "v")], [(0, 512, "s"), (512, 256, "v")]]
-        for a in range(2, A):
-            chunks.append([(0, 512, "s"), (512, 256, "s")])
+        chunks = [
+            [(0, 256, "v"), (256, 256, "s"), (512, 128, "v"), (640, 128, "s")],
+            [(0, 512, "s"), (512, 256, "v")],
+            [(0, 512, "s"), (512, 256, "s")],
+            [(0, 512, "s"), (512, 256, "s")],
+            [(0, 512, "s"), (512, 256, "s")],
+        ]
+        loads = [((0, 512), (512, 768)), ((0, 768),), ((0, 768),), ((0, 768),), ((0, 512), (512, 768))]
 
         nc.sync.dma_start(offs_t[:], offs)
         raws = {}
-        for a in range(A):
+
+        def load(a):
             rows = xT[512 * a : 512 * (a + 1), :].rearrange("(p j) w -> p j w", j=4)
-            for t0, tn, eng in chunks[a]:
-                raw = held([P, 4, tn], F32, "raw_%d_%d" % (a, t0))
-                nc.sync.dma_start(out=raw[:], in_=rows[:, :, t0 : t0 + tn])
-                raws[(a, t0)] = raw
+            for t0, t1 in loads[a]:
+                raw = held([P, 4, t1 - t0], F32, "raw_%d_%d" % (a, t0))
+                nc.sync.dma_start(out=raw[:], in_=rows[:, :, t0:t1])
+                for c0, cn, eng in chunks[a]:
+                    if t0 <= c0 < t1:
+                        raws[(a, c0)] = raw[:, :, c0 - t0 : c0 - t0 + cn]
+
+        for a in range(4):
+            load(a)
 
         words = held([P, E * A * 2 * N], U8, "words")
         wplane = held([P, E * A * N], U8, "wplane")
@@ -66,10 +77,13 @@ def tile_moe_rag_lin_bias_kernel(tc, xT, w_words, w_scales, b, gate, offs, pos1,
                 out=wplane[32 * q : 32 * q + 4, :].bitcast(I32).rearrange("r (m c) -> r m c", m=E * A),
                 in_=w_scales[:, :, 4 * q : 4 * q + 4, :].bitcast(I32).rearrange("e a r c -> r (e a) c"),
             )
-        nc.sync.dma_start(
-            out=words[:].bitcast(I32).rearrange("p (m c) -> p m c", m=E * A),
-            in_=w_words.bitcast(I32).rearrange("e a p c -> p (e a) c"),
-        )
+        for e0, e1 in ((3, 6), (0, 3)):
+            nc.sync.dma_start(
+                out=words[:, 2 * N * A * e0 : 2 * N * A * e1].bitcast(I32).rearrange("p (m c) -> p m c", c=N // 2),
+                in_=w_words[e0:e1].bitcast(I32).rearrange("e a p c -> p (e a) c"),
+            )
+            if e0 == 3:
+                load(4)
         gates = []
         for c in range(2):
             g_t = held([P, T], F32, "gate_%d" % c)
@@ -91,7 +105,7 @@ def tile_moe_rag_lin_bias_kernel(tc, xT, w_words, w_scales, b, gate, offs, pos1,
         def cast(a):
             for t0, tn, eng in chunks[a]:
                 grouped = held([P, tn, 4], BF16, "grouped_%d_%d" % (a, t0))
-                src = raws[(a, t0)][:].rearrange("p j w -> p w j")
+                src = raws[(a, t0)].rearrange("p j w -> p w j")
                 if eng == "v":
                     nc.vector.tensor_copy(out=grouped[:], in_=src)
                 else:
@@ -171,8 +185,8 @@ def tile_moe_rag_lin_bias_kernel(tc, xT, w_words, w_scales, b, gate, offs, pos1,
             nc.sync.dma_start(out=moved[a][0 : P - 4 * a, :].bitcast(I32), in_=gpacked[4 * a : P, :].bitcast(I32))
         for s0, s1 in thirds:
             gather(gwords[3], codes[3], s0, s1)
-        for a in range(4):
-            for blk in early:
+        for blk in early:
+            for a in range(4):
                 multiply(a, blk)
         quantize(4)
 

from contextlib import ExitStack

import concourse.mybir as mybir

FLOPS = 2 * 1536 * 2560 * 128

F32 = mybir.dt.float32
BF16 = mybir.dt.bfloat16
I32 = mybir.dt.int32
U32 = mybir.dt.uint32
U16 = mybir.dt.uint16
U8 = mybir.dt.uint8
FP8X4 = mybir.dt.float8_e4m3fn_x4
FP4X4 = mybir.dt.float4_e2m1fn_x4
MULT = mybir.AluOpType.mult
IDENTITY = mybir.ActivationFunctionType.Identity

P = 128
T = 768
S = 1536
E = 6
N = 128
A = 5


def tile_moe_rag_lin_bias_kernel(tc, xT, w_words, w_scales, b, gate, offs, pos1, pos2, out):
    nc = tc.nc
    with ExitStack() as ctx:
        pool = ctx.enter_context(tc.tile_pool(name="held", bufs=1))
        psum = ctx.enter_context(tc.psum_pool(name="psum", bufs=1))

        def held(shape, dtype, name):
            return pool.tile(shape, dtype, name=name, align_bytes=64)

        offs_t = held([P, S // 16], U16, "offs_t")
        pos1_t = held([P, T // 16], U16, "pos1_t")
        pos2_t = held([P, T // 16], U16, "pos2_t")

        chunks = [
            [(0, 256, "v"), (256, 256, "s"), (512, 128, "v"), (640, 128, "s")],
            [(0, 512, "s"), (512, 256, "v")],
            [(0, 512, "s"), (512, 256, "s")],
            [(0, 512, "s"), (512, 256, "s")],
            [(0, 512, "s"), (512, 256, "s")],
        ]
        loads = [((0, 512), (512, 768)), ((0, 768),), ((0, 768),), ((0, 768),), ((0, 512), (512, 768))]

        nc.sync.dma_start(offs_t[:], offs)
        raws = {}

        def load(a):
            rows = xT[512 * a : 512 * (a + 1), :].rearrange("(p j) w -> p j w", j=4)
            for t0, t1 in loads[a]:
                raw = held([P, 4, t1 - t0], F32, "raw_%d_%d" % (a, t0))
                nc.sync.dma_start(out=raw[:], in_=rows[:, :, t0:t1])
                for c0, cn, eng in chunks[a]:
                    if t0 <= c0 < t1:
                        raws[(a, c0)] = raw[:, :, c0 - t0 : c0 - t0 + cn]

        for a in range(4):
            load(a)

        words = held([P, E * A * 2 * N], U8, "words")
        wplane = held([P, E * A * N], U8, "wplane")
        lone = held([P, T], U8, "lone")
        packed = held([P, T], U8, "packed")
        moved = {}
        for a in (1, 2, 3):
            moved[a] = held([P, S], U8, "moved_%d" % a)
        for plane in (packed, lone, wplane, moved[1], moved[2], moved[3]):
            nc.gpsimd.memset(plane[:].bitcast(I32), 0)

        b_t = held([P, E], F32, "b_t")
        nc.sync.dma_start(out=b_t[:], in_=b)
        for q in range(4):
            nc.sync.dma_start(
                out=wplane[32 * q : 32 * q + 4, :].bitcast(I32).rearrange("r (m c) -> r m c", m=E * A),
                in_=w_scales[:, :, 4 * q : 4 * q + 4, :].bitcast(I32).rearrange("e a r c -> r (e a) c"),
            )
        for e0, e1 in ((3, 6), (0, 3)):
            nc.sync.dma_start(
                out=words[:, 2 * N * A * e0 : 2 * N * A * e1].bitcast(I32).rearrange("p (m c) -> p m c", c=N // 2),
                in_=w_words[e0:e1].bitcast(I32).rearrange("e a p c -> p (e a) c"),
            )
            if e0 == 3:
                load(4)
        gates = []
        for c in range(2):
            g_t = held([P, T], F32, "gate_%d" % c)
            nc.sync.dma_start(out=g_t[:], in_=gate[c])
            gates.append(g_t)
        nc.sync.dma_start(pos1_t[:], pos1)
        nc.sync.dma_start(pos2_t[:], pos2)

        codes = {}
        gwords = {}
        for a in range(A):
            codes[a] = held([P, T], U32, "codes_%d" % a)
            gwords[a] = held([P, S], U32, "gwords_%d" % a)
        glone = held([P, S], U8, "glone")
        gpacked = held([P, S], U8, "gpacked")

        groups = {}

        def cast(a):
            for t0, tn, eng in chunks[a]:
                grouped = held([P, tn, 4], BF16, "grouped_%d_%d" % (a, t0))
                src = raws[(a, t0)].rearrange("p j w -> p w j")
                if eng == "v":
                    nc.vector.tensor_copy(out=grouped[:], in_=src)
                else:
                    nc.scalar.copy(out=grouped[:], in_=src)
                groups[(a, t0)] = grouped

        def quantize(a):
            for t0, tn, eng in chunks[a]:
                plane = lone[:, t0 : t0 + tn] if a == A - 1 else packed[4 * a : P, t0 : t0 + tn]
                nc.vector.quantize_mx(
                    out=codes[a][:, t0 : t0 + tn].bitcast(FP8X4),
                    scales=plane,
                    in_=groups[(a, t0)][:].rearrange("p w j -> p (w j)"),
                )

        def gather(dst, src, s0, s1):
            nc.vector.tensor_copy(dst[:, s0:s1], src[:].indirect(offs_t[:, s0 // 16 : s1 // 16]))

        planes = {0: gpacked, 1: moved[1], 2: moved[2], 3: moved[3], 4: glone}

        blocks = [
            (7, 0, 5, 1024, 512),
            (4, 0, 3, 512, 128),
            (5, 0, 4, 640, 128),
            (6, 0, 4, 768, 128),
            (6, 128, 4, 896, 128),
            (1, 0, 1, 128, 128),
            (2, 0, 2, 256, 128),
            (3, 0, 3, 384, 128),
            (0, 0, 0, 0, 128),
        ]
        early = [blk for blk in blocks if blk[1] == 0]
        banks = []
        for i in range(8):
            banks.append(psum.tile([P, 512], F32, name="bank_%d" % i))
        y = held([P, S], F32, "y")

        def multiply(a, block):
            bank, col, e, s0, sn = block
            m = e * A + a
            nc.tensor.matmul_mx(
                out=banks[bank][:, col : col + sn],
                lhsT=words[:, 2 * N * m : 2 * N * (m + 1)].bitcast(FP4X4),
                lhsT_scale=wplane[:, N * m : N * (m + 1)],
                rhs=gwords[a][:, s0 : s0 + sn].bitcast(FP8X4),
                rhs_scale=planes[a][:, s0 : s0 + sn],
                start=(a == 0),
                stop=(a == A - 1),
            )

        def leave(bank, col, e, s0, sn):
            if s0 == 0:
                nc.vector.tensor_scalar_add(out=y[:, s0 : s0 + sn], in0=banks[bank][:, col : col + sn], scalar1=b_t[:, e : e + 1])
            else:
                nc.scalar.activation(out=y[:, s0 : s0 + sn], in_=banks[bank][:, col : col + sn], func=IDENTITY, bias=b_t[:, e : e + 1])

        thirds = ((0, 512), (512, 1024), (1024, 1536))

        cast(0)
        cast(1)
        quantize(0)
        for s0, s1 in thirds:
            gather(gwords[0], codes[0], s0, s1)
        cast(2)
        quantize(1)
        for s0, s1 in thirds:
            gather(gwords[1], codes[1], s0, s1)
        cast(3)
        quantize(2)
        for s0, s1 in thirds:
            gather(gwords[2], codes[2], s0, s1)
        cast(4)
        quantize(3)
        for s0, s1 in thirds:
            gather(gpacked, packed, s0, s1)
        for a in (1, 2, 3):
            nc.sync.dma_start(out=moved[a][0 : P - 4 * a, :].bitcast(I32), in_=gpacked[4 * a : P, :].bitcast(I32))
        for s0, s1 in thirds:
            gather(gwords[3], codes[3], s0, s1)
        for blk in early:
            for a in range(4):
                multiply(a, blk)
        quantize(4)

        for s0, s1 in ((1024, 1536), (512, 1024), (128, 512), (0, 128)):
            gather(glone, lone, s0, s1)
            gather(gwords[4], codes[4], s0, s1)
            for blk in blocks:
                if s0 <= blk[3] < s1:
                    if blk[1] > 0:
                        for a in range(A - 1):
                            multiply(a, blk)
                    multiply(4, blk)
                    if blk[0] == 6:
                        if blk[1] > 0:
                            leave(6, 0, 4, 768, 256)
                    else:
                        leave(*blk)

        terms = {}

        def fetch(c, t0, t1):
            pos = (pos1_t, pos2_t)[c]
            term = held([P, t1 - t0], F32, "term_%d_%d" % (c, t0))
            nc.vector.tensor_tensor(term[:], y[:].indirect(pos[:, t0 // 16 : t1 // 16]), gates[c][:, t0:t1], MULT)
            terms[(c, t0)] = term

        def finish(t0, t1):
            total = held([P, t1 - t0], F32, "total_%d" % t0)
            nc.vector.tensor_add(out=total[:], in0=terms[(0, t0)][:], in1=terms[(1, t0)][:])
            nc.sync.dma_start(out=out[:, t0:t1], in_=total[:])

        fetch(0, 0, 512)
        fetch(1, 0, 512)
        fetch(0, 512, 768)
        finish(0, 512)
        fetch(1, 512, 768)
        finish(512, 768)
